import numpy as np
import ml_dtypes


def mxq(x, axis, fmt="e4m3"):
    dtype, down = {"e4m3": (ml_dtypes.float8_e4m3fn, 7), "e5m2": (ml_dtypes.float8_e5m2, 14)}[fmt]
    v = np.moveaxis(np.asarray(x, np.float32).astype(ml_dtypes.bfloat16).astype(np.float64), axis, -1)
    blocks = v.reshape(v.shape[:-1] + (-1, 32))
    amax = np.abs(blocks).max(-1, keepdims=True)
    byte = np.maximum(np.where(amax > 0, np.frexp(amax)[1] - 1 + 127, 0) - down, 1)
    scale = np.exp2(byte - 127.0)
    codes = (blocks / scale).astype(np.float32).astype(dtype).astype(np.float64)
    return np.moveaxis((codes * scale).reshape(v.shape), -1, axis)


WIDE = False


def mx_kscale(k):
    if not WIDE:
        return np.ones(k)
    levels = np.array([10, -10, 5, -5, 0])
    if k % 512:
        return np.exp2(np.random.permutation(np.resize(levels, k // 32))).repeat(32)
    a = np.empty((k // 512, 16))
    for p in range(k // 512):
        a[p, :8] = np.random.permutation(np.resize(levels, 8))
        for g in range(8):
            far = levels[np.abs(levels - a[p, g]) >= 10]
            a[p, g + 8] = far[np.random.randint(len(far))]
    return np.exp2(a.ravel()).repeat(32)


def f64(x):
    return np.asarray(x).astype(np.float64)


def striped(idx):
    return np.tile(idx.reshape(-1, 16).T, (8, 1)).astype(np.uint16)


def unstriped(offs):
    return offs[:16].T.reshape(-1).astype(np.int64)


E2M1 = np.array([0.0, 0.5, 1.0, 1.5, 2.0, 3.0, 4.0, 6.0, -0.0, -0.5, -1.0, -1.5, -2.0, -3.0, -4.0, -6.0])


def pack_weight(w, fmt):
    k, n = w.shape
    w = f64(np.asarray(w, np.float32).astype(ml_dtypes.bfloat16)).reshape(k // 32, 32, n)
    amax = np.abs(w).max(1)
    if fmt == "e4m3":
        byte = np.frexp(amax)[1] - 1 + 127 - 7
    else:
        mant, ex = np.frexp(amax / 6.0)
        byte = np.where(mant > 0.5, ex, ex - 1) + 127
    byte = np.clip(np.where(amax > 0, byte, 1), 1, 254)
    scaled = (w * np.exp2(127.0 - byte)[:, None, :]).reshape(k, n).astype(np.float32)
    by_word = np.ascontiguousarray(scaled.reshape(k // 512, 128, 4, n).transpose(0, 1, 3, 2))
    if fmt == "e4m3":
        words = by_word.astype(ml_dtypes.float8_e4m3fn).view(np.uint8)
    else:
        c = by_word.astype(ml_dtypes.float4_e2m1fn).view(np.uint8) & 0xF
        words = (c[..., 0::2] | (c[..., 1::2] << 4)).reshape(k // 512, 128, 2 * n)
    return np.ascontiguousarray(words), np.ascontiguousarray(byte.astype(np.uint8).reshape(k // 512, 16, n))


def unpack_weight(words, scales, fmt):
    g, _, n = scales.shape
    words = np.ascontiguousarray(words).reshape(g, 128, n, -1)
    if fmt == "e4m3":
        vals = words.view(ml_dtypes.float8_e4m3fn).astype(np.float64)
    else:
        nib = np.empty((g, 128, n, 4), np.uint8)
        nib[..., 0::2] = words & 0xF
        nib[..., 1::2] = words >> 4
        vals = E2M1[nib]
    vals = vals * np.repeat(np.exp2(scales.astype(np.float64) - 127.0), 8, axis=1)[..., None]
    return vals.transpose(0, 1, 3, 2).reshape(g * 512, n)


def gelu(v):
    return 0.5 * v * (1.0 + np.tanh(np.sqrt(2.0 / np.pi) * (v + 0.044715 * v**3)))


K, H, N, T, S, P = 1536, 1024, 512, 2048, 1024, 512

def setup_inputs():
    n = np.random.standard_normal
    s = mx_kscale(K)[:, None]
    u = mx_kscale(H)[:, None]
    tab_words, tab_scales = pack_weight(n((K, T)) * s, "e4m3")
    wl_words, wl_scales = pack_weight(n((H, N)) / np.sqrt(H) / u, "e2m1")
    return {
        "tab_words": tab_words, "tab_scales": tab_scales,
        "offs": striped(np.random.permutation(T)[:S]),
        "pos1": striped(np.random.permutation(S)[:P]),
        "pos2": striped(np.random.permutation(S)[:P]),
        "w1": (n((K, H)) / np.sqrt(K) / s * u.T).astype(np.float32),
        "wl_words": wl_words, "wl_scales": wl_scales,
        "we": (n((H, N)) / np.sqrt(H) / u).astype(np.float32),
    }

def reference(tab_words, tab_scales, offs, pos1, pos2, w1, wl_words, wl_scales, we):
    v = unpack_weight(tab_words, tab_scales, "e4m3")[:, unstriped(offs)]
    h = np.maximum(mxq(f64(w1), 0, "e4m3").T @ v, 0.0)
    z = h[:, unstriped(pos1)] + h[:, unstriped(pos2)]
    zq = mxq(z, 0, "e4m3")
    wl = unpack_weight(wl_words, wl_scales, "e2m1")
    loss = wl.T @ zq
    expo = mxq(f64(we), 0, "e4m3").T @ zq
    return loss / (1.0 + np.abs(expo))

@@ -1,0 +1,296 @@
+from contextlib import ExitStack
+
+import concourse.mybir as mybir
+
+K, H, N, T, S, J = 1536, 1024, 512, 2048, 1024, 512
+FLOPS = 2 * K * H * S + 2 * 2 * H * N * J
+
+F32 = mybir.dt.float32
+BF16 = mybir.dt.bfloat16
+I32 = mybir.dt.int32
+U32 = mybir.dt.uint32
+U16 = mybir.dt.uint16
+U8 = mybir.dt.uint8
+FP8X4 = mybir.dt.float8_e4m3fn_x4
+FP4X4 = mybir.dt.float4_e2m1fn_x4
+ACT = mybir.ActivationFunctionType
+ALU = mybir.AluOpType
+
+P = 128
+PACK = 4
+PASS = P * PACK
+BANK = 512
+KP = K // PASS
+RP = H // PASS
+NT = N // P
+UNIT = 128
+LANES = 16
+HALF = PASS // 2
+WIDE = PASS * PACK
+LAP = 32
+
+
+def tile_list_guarantor_loss_rates_kernel(
+    tc, tab_words, tab_scales, offs, pos1, pos2, w1, wl_words, wl_scales, we, out
+):
+    nc = tc.nc
+    with ExitStack() as ctx:
+        keep = ctx.enter_context(tc.tile_pool(name="keep", bufs=1))
+        ring = ctx.enter_context(tc.tile_pool(name="ring", bufs=2))
+        psum = ctx.enter_context(tc.psum_pool(name="psum", bufs=8))
+
+        offs_sb = keep.tile([P, S // LANES], U16, name="offs_sb")
+        pos1_sb = keep.tile([P, J // LANES], U16, name="pos1_sb")
+        pos2_sb = keep.tile([P, J // LANES], U16, name="pos2_sb")
+
+        tab_w = [keep.tile([P, T], I32, name=f"tab_w{a}") for a in range(KP)]
+        tab_s = keep.tile([P, T // 4], I32, name="tab_s")
+        v_w = [keep.tile([P, S], U32, name=f"v_w{a}", align_bytes=64) for a in range(KP - 1)]
+        v_s = keep.tile([P, S], U8, name="v_s", align_bytes=64)
+
+        wl_w = keep.tile([P, RP, N // 2], I32, name="wl_w", align_bytes=64)
+        wl_s = keep.tile([P, RP, N // 4], I32, name="wl_s", align_bytes=64)
+
+        nc.vector.memset(tab_s[:], 0)
+        nc.vector.memset(wl_s[:], 0)
+
+        def load_tab(a):
+            nc.sync.dma_start(tab_w[a][:], tab_words[a].rearrange("p n i -> p (n i)").bitcast(I32))
+
+        w1_raw = {}
+
+        def load_w1(a, b, c0, c1):
+            raw = keep.tile([P, PACK, c1 - c0], F32, name=f"w1_raw{a}{b}{c0}")
+            src = w1[a * PASS : (a + 1) * PASS, b * PASS + c0 : b * PASS + c1]
+            nc.sync.dma_start(raw[:], src.rearrange("(p j) c -> p j c", j=PACK))
+            w1_raw[a, b, c0] = raw
+
+        load_tab(0)
+        nc.sync.dma_start(offs_sb[:], offs)
+        for q in range(4):
+            nc.scalar.dma_start(
+                tab_s[32 * q : 32 * q + 4 * KP, :], tab_scales[:, 4 * q : 4 * q + 4, :].bitcast(I32)
+            )
+        warm_in = keep.tile([P, 1], F32, name="warm_in")
+        warm_out = keep.tile([P, 1], F32, name="warm_out")
+        nc.vector.memset(warm_in[:], 1.0)
+        nc.scalar.activation(warm_out[:], warm_in[:], ACT.Abs_reciprocal_sqrt)
+        load_w1(0, 0, 0, PASS)
+        load_tab(1)
+        load_tab(2)
+        for a in (1, 2):
+            load_w1(a, 0, 0, HALF)
+            load_w1(a, 0, HALF, PASS)
+        nc.sync.dma_start(pos1_sb[:], pos1)
+        nc.sync.dma_start(pos2_sb[:], pos2)
+        for a in range(KP):
+            load_w1(a, 1, 0, PASS)
+        we_raw = []
+        for b in range(RP):
+            raw = keep.tile([P, PACK, N], F32, name=f"we_raw{b}")
+            nc.sync.dma_start(raw[:], we[b * PASS : (b + 1) * PASS, :].rearrange("(p j) n -> p j n", j=PACK))
+            we_raw.append(raw)
+        nc.sync.dma_start(wl_w[:], wl_words.bitcast(I32).rearrange("a p c -> p a c"))
+        for q in range(4):
+            nc.sync.dma_start(
+                wl_s[32 * q : 32 * q + 4, :, :],
+                wl_scales[:, 4 * q : 4 * q + 4, :].bitcast(I32).rearrange("a i c -> i a c"),
+            )
+
+        def tile(shape, dtype, name, tag=None):
+            return keep.tile(shape, dtype, name=name, tag=tag or name, align_bytes=64)
+
+        h = {(b, t): tile([P, S], F32, f"h{b}{t}") for b in range(RP) for t in range(PACK)}
+        w1_w, w1_s = {}, {}
+
+        def quantize(codes, scales, src):
+            nc.vector.quantize_mx(out=codes.bitcast(FP8X4), scales=scales, in_=src)
+
+        def round_w1(copy, grouped, a, b, c0, lo, hi):
+            raw = w1_raw[a, b, c0]
+            copy(
+                grouped.rearrange("p (t m j) -> p m j t", t=PACK, j=PACK)[:, lo // PACK : hi // PACK],
+                raw[:, :, lo - c0 : hi - c0].rearrange("p j (m t) -> p m j t", t=PACK),
+            )
+
+        def quantize_w1(grouped, a, b):
+            codes = tile([P, PASS], U32, f"w1_w{a}{b}")
+            scales = tile([P, PASS], U8, f"w1_s{a}{b}")
+            quantize(codes[:], scales[:], grouped)
+            for t in range(PACK):
+                w1_w[a, b, t] = codes[:, t * P : (t + 1) * P]
+                w1_s[a, b, t] = scales[:, t * P : (t + 1) * P]
+
+        def quantize_w1_by_t(grouped, a, b):
+            for t in range(PACK):
+                codes = tile([P, P], U32, f"w1_w{a}{b}{t}")
+                scales = tile([P, P], U8, f"w1_s{a}{b}{t}")
+                quantize(codes[:], scales[:], grouped[:, t * PASS : (t + 1) * PASS])
+                w1_w[a, b, t], w1_s[a, b, t] = codes[:], scales[:]
+
+        def layer1_pass(banks, a, b, t):
+            for half in range(S // BANK):
+                ent = slice(half * BANK, (half + 1) * BANK)
+                nc.tensor.matmul_mx(
+                    out=banks[t, half][:],
+                    lhsT=w1_w[a, b, t].bitcast(FP8X4),
+                    lhsT_scale=w1_s[a, b, t],
+                    rhs=v_w[a][:, ent].bitcast(FP8X4),
+                    rhs_scale=v_s[4 * a : P, ent],
+                    start=(a == 0),
+                    stop=(a == KP - 1),
+                )
+
+        def relu_out(banks, b, t, half, on_vector):
+            dst = h[b, t][:, half * BANK : (half + 1) * BANK]
+            if on_vector:
+                nc.vector.tensor_scalar_max(dst, banks[t, half][:], 0.0)
+            else:
+                nc.scalar.activation(dst, banks[t, half][:], ACT.Relu)
+
+        def new_banks():
+            return {(t, half): psum.tile([P, BANK], F32, name="bank") for t in range(PACK) for half in range(S // BANK)}
+
+        z_w = [tile([P, J], U32, f"z_w{b}") for b in range(RP)]
+        z_s = [tile([P, J], U8, f"z_s{b}") for b in range(RP)]
+
+        def pick(picked, b, t, j0, j1):
+            for side, lst in enumerate((pos1_sb, pos2_sb)):
+                nc.vector.tensor_copy(picked[:, side, t, :], h[b, t][:].indirect(lst[:, j0 // LANES : j1 // LANES]))
+
+        def add_z(z_bf, picked, c0, c1):
+            nc.vector.tensor_tensor(
+                z_bf.rearrange("p (c i t) -> p c t i", i=4, t=PACK),
+                picked[:, 0, :, c0:c1].rearrange("p t (c i) -> p c t i", i=4),
+                picked[:, 1, :, c0:c1].rearrange("p t (c i) -> p c t i", i=4),
+                ALU.add,
+            )
+
+        def quantize_z(z_bf, b, j0, j1):
+            quantize(z_w[b][:, j0:j1], z_s[b][:, j0:j1], z_bf)
+
+        def gather_words(a):
+            nc.vector.tensor_copy(v_w[a][:], tab_w[a][:].bitcast(U32).indirect(offs_sb[:]))
+
+        banks = new_banks()
+        gather_words(0)
+        nc.vector.tensor_copy(v_s[:], tab_s[:].bitcast(U8).indirect(offs_sb[:]))
+        gather_words(1)
+        grouped00 = tile([P, WIDE], BF16, "grouped00", tag="slot_a")
+        round_w1(nc.scalar.copy, grouped00[:], 0, 0, 0, 0, PASS)
+        quantize_w1(grouped00[:], 0, 0)
+        for t in range(PACK):
+            layer1_pass(banks, 0, 0, t)
+        v_w.append(tile([P, S], U32, "v_w2", tag="slot_a"))
+        gather_words(2)
+
+        pair = tile([P, 2 * WIDE - LAP], BF16, "pair")
+        grouped10 = pair[:, WIDE - LAP :]
+        grouped20 = pair[:, :WIDE]
+        round_w1(nc.scalar.copy, grouped10, 1, 0, 0, 0, HALF)
+        round_w1(nc.scalar.copy, grouped10, 1, 0, HALF, HALF, PASS)
+        quantize_w1(grouped10, 1, 0)
+        round_w1(nc.scalar.copy, grouped20, 2, 0, 0, 0, HALF)
+        round_w1(nc.vector.tensor_copy, grouped20, 2, 0, HALF, HALF, PASS)
+        quantize_w1_by_t(grouped20, 2, 0)
+
+        picked0 = tile([P, 2, PACK, J], F32, "picked0", tag="slot_p")
+
+        def finish0(t):
+            relu_out(banks, 0, t, 0, False)
+            relu_out(banks, 0, t, 1, t == 0)
+            pick(picked0, 0, t, 0, J)
+
+        for t in range(PACK):
+            layer1_pass(banks, 1, 0, t)
+            layer1_pass(banks, 2, 0, t)
+        for t in range(PACK - 1):
+            finish0(t)
+
+        banks1 = new_banks()
+        grouped01 = tile([P, WIDE], BF16, "grouped01", tag="w1_w201")
+        round_w1(nc.scalar.copy, grouped01[:], 0, 1, 0, 0, PASS)
+        quantize_w1(grouped01[:], 0, 1)
+        finish0(PACK - 1)
+        for t in range(PACK):
+            layer1_pass(banks1, 0, 1, t)
+
+        both11 = tile([P, WIDE + WIDE // 2 - LAP], BF16, "both11", tag="w1_w202")
+        round_w1(nc.scalar.copy, both11[:, :WIDE], 1, 1, 0, 0, PASS)
+        quantize_w1(both11[:, :WIDE], 1, 1)
+        both21 = tile([P, WIDE + WIDE // 2 - LAP], BF16, "both21", tag="w1_w203")
+        round_w1(nc.scalar.copy, both21[:, :WIDE], 2, 1, 0, 0, PASS)
+        quantize_w1_by_t(both21[:, :WIDE], 2, 1)
+        add_z(both11[:, WIDE - LAP :], picked0, 0, J // 2)
+        add_z(both21[:, WIDE - LAP :], picked0, J // 2, J)
+        quantize_z(both11[:, WIDE - LAP :], 0, 0, J // 2)
+        quantize_z(both21[:, WIDE - LAP :], 0, J // 2, J)
+
+        z_bf1 = tile([P, J * PACK], BF16, "z_bf1")
+        picked = tile([P, 2, PACK, 2 * UNIT], F32, "picked10", tag="slot_p")
+        for t in range(PACK):
+            layer1_pass(banks1, 1, 1, t)
+            layer1_pass(banks1, 2, 1, t)
+            relu_out(banks1, 1, t, 0, False)
+            relu_out(banks1, 1, t, 1, False)
+            pick(picked, 1, t, 0, 2 * UNIT)
+        add_z(z_bf1[:, : 2 * UNIT * PACK], picked, 0, 2 * UNIT)
+        quantize_z(z_bf1[:, : 2 * UNIT * PACK], 1, 0, 2 * UNIT)
+
+        we_w = [tile([P, N], U32, f"we_w{b}") for b in range(RP)]
+        we_s = [tile([P, N], U8, f"we_s{b}") for b in range(RP)]
+        for b in range(RP):
+            grouped = tile([P, N * PACK], BF16, f"grouped_we{b}", tag=f"w1_s20{3 - b}")
+            for n0 in (0, N // 2):
+                nc.scalar.copy(
+                    grouped[:, PACK * n0 : PACK * (n0 + N // 2)].rearrange("p (c i j) -> p c j i", i=4, j=PACK),
+                    we_raw[b][:, :, n0 : n0 + N // 2].rearrange("p j (c i) -> p c j i", i=4),
+                )
+            quantize(we_w[b][:], we_s[b][:], grouped[:])
+
+        out_v = out.rearrange("(nt p) j -> p nt j", p=P)
+
+        def heads(u):
+            cols = slice(u * UNIT, (u + 1) * UNIT)
+            expo = psum.tile([P, BANK], F32, name="bank")
+            loss = psum.tile([P, BANK], F32, name="bank")
+            for nt in range(NT):
+                for b in range(RP):
+                    nc.tensor.matmul_mx(
+                        out=expo[:, nt * UNIT : (nt + 1) * UNIT],
+                        lhsT=we_w[b][:, nt * P : (nt + 1) * P].bitcast(FP8X4),
+                        lhsT_scale=we_s[b][:, nt * P : (nt + 1) * P],
+                        rhs=z_w[b][:, cols].bitcast(FP8X4),
+                        rhs_scale=z_s[b][:, cols],
+                        start=(b == 0),
+                        stop=(b == RP - 1),
+                    )
+            for nt in range(NT):
+                for b in range(RP):
+                    nc.tensor.matmul_mx(
+                        out=loss[:, nt * UNIT : (nt + 1) * UNIT],
+                        lhsT=wl_w[:, b, :].bitcast(U8)[:, 2 * nt * P : 2 * (nt + 1) * P].bitcast(FP4X4),
+                        lhsT_scale=wl_s[:, b, :].bitcast(U8)[:, nt * P : (nt + 1) * P],
+                        rhs=z_w[b][:, cols].bitcast(FP8X4),
+                        rhs_scale=z_s[b][:, cols],
+                        start=(b == 0),
+                        stop=(b == RP - 1),
+                    )
+            size = ring.tile([P, BANK], F32, name="size")
+            root = ring.tile([P, BANK], F32, name="root")
+            score = keep.tile([P, BANK], F32, name=f"score{u}")
+            nc.scalar.activation(size[:], expo[:], ACT.Abs)
+            nc.scalar.activation(root[:], size[:], ACT.Abs_reciprocal_sqrt, bias=1.0)
+            nc.scalar.activation(size[:], root[:], ACT.Square)
+            nc.vector.tensor_tensor(score[:], loss[:], size[:], ALU.mult)
+            nc.sync.dma_start(out_v[:, :, cols], score[:].rearrange("p (nt j) -> p nt j", nt=NT))
+
+        for u in (2, 3):
+            j0, j1 = u * UNIT, (u + 1) * UNIT
+            picked = tile([P, 2, PACK, UNIT], F32, f"picked1{u}", tag="w1_s202")
+            for t in range(PACK):
+                pick(picked, 1, t, j0, j1)
+            add_z(z_bf1[:, j0 * PACK : j1 * PACK], picked, 0, UNIT)
+            quantize_z(z_bf1[:, j0 * PACK : j1 * PACK], 1, j0, j1)
+        for u in range(J // UNIT):
+            heads(u)

@@ -1,6 +1,7 @@
 from contextlib import ExitStack
 
 import concourse.mybir as mybir
+from concourse.masks import make_identity
 
 K, H, N, T, S, J = 1536, 1024, 512, 2048, 1024, 512
 FLOPS = 2 * K * H * S + 2 * 2 * H * N * J
@@ -37,15 +38,15 @@ def tile_list_guarantor_loss_rates_kernel(
     with ExitStack() as ctx:
         keep = ctx.enter_context(tc.tile_pool(name="keep", bufs=1))
         ring = ctx.enter_context(tc.tile_pool(name="ring", bufs=2))
-        psum = ctx.enter_context(tc.psum_pool(name="psum", bufs=8))
+        psum = ctx.enter_context(tc.psum_pool(name="psum", bufs=1))
 
         offs_sb = keep.tile([P, S // LANES], U16, name="offs_sb")
         pos1_sb = keep.tile([P, J // LANES], U16, name="pos1_sb")
         pos2_sb = keep.tile([P, J // LANES], U16, name="pos2_sb")
 
-        tab_w = [keep.tile([P, T], I32, name=f"tab_w{a}") for a in range(KP)]
+        tab_w = [keep.tile([P, T], I32, name=f"tab_w{a}", tag=f"tab_w{a}", align_bytes=64) for a in range(KP)]
         tab_s = keep.tile([P, T // 4], I32, name="tab_s")
-        v_w = [keep.tile([P, S], U32, name=f"v_w{a}", align_bytes=64) for a in range(KP - 1)]
+        v_w = {}
         v_s = keep.tile([P, S], U8, name="v_s", align_bytes=64)
 
         wl_w = keep.tile([P, RP, N // 2], I32, name="wl_w", align_bytes=64)
@@ -60,7 +61,7 @@ def tile_list_guarantor_loss_rates_kernel(
         w1_raw = {}
 
         def load_w1(a, b, c0, c1):
-            raw = keep.tile([P, PACK, c1 - c0], F32, name=f"w1_raw{a}{b}{c0}")
+            raw = keep.tile([P, PACK, c1 - c0], F32, name=f"w1_raw{a}{b}{c0}", tag=f"w1_raw{a}{b}{c0}", align_bytes=64)
             src = w1[a * PASS : (a + 1) * PASS, b * PASS + c0 : b * PASS + c1]
             nc.sync.dma_start(raw[:], src.rearrange("(p j) c -> p j c", j=PACK))
             w1_raw[a, b, c0] = raw
@@ -68,26 +69,32 @@ def tile_list_guarantor_loss_rates_kernel(
         load_tab(0)
         nc.sync.dma_start(offs_sb[:], offs)
         for q in range(4):
-            nc.scalar.dma_start(
+            (nc.sync, nc.scalar)[q % 2].dma_start(
                 tab_s[32 * q : 32 * q + 4 * KP, :], tab_scales[:, 4 * q : 4 * q + 4, :].bitcast(I32)
             )
         warm_in = keep.tile([P, 1], F32, name="warm_in")
         warm_out = keep.tile([P, 1], F32, name="warm_out")
         nc.vector.memset(warm_in[:], 1.0)
         nc.scalar.activation(warm_out[:], warm_in[:], ACT.Abs_reciprocal_sqrt)
-        load_w1(0, 0, 0, PASS)
+        ident = keep.tile([P, P], F32, name="ident")
+        make_identity(nc, ident[:])
+        load_w1(0, 0, 0, HALF)
         load_tab(1)
+        load_w1(1, 0, 0, HALF)
         load_tab(2)
-        for a in (1, 2):
-            load_w1(a, 0, 0, HALF)
-            load_w1(a, 0, HALF, PASS)
+        load_w1(2, 0, 0, HALF)
+        load_w1(0, 0, HALF, PASS)
         nc.sync.dma_start(pos1_sb[:], pos1)
         nc.sync.dma_start(pos2_sb[:], pos2)
-        for a in range(KP):
-            load_w1(a, 1, 0, PASS)
+        load_w1(1, 0, HALF, PASS)
+        load_w1(2, 0, HALF, PASS)
+        load_w1(0, 1, 0, HALF)
+        load_w1(0, 1, HALF, PASS)
+        load_w1(1, 1, 0, PASS)
+        load_w1(2, 1, 0, PASS)
         we_raw = []
         for b in range(RP):
-            raw = keep.tile([P, PACK, N], F32, name=f"we_raw{b}")
+            raw = keep.tile([P, PACK, N], F32, name=f"we_raw{b}", tag=f"we_raw{b}", align_bytes=64)
             nc.sync.dma_start(raw[:], we[b * PASS : (b + 1) * PASS, :].rearrange("(p j) n -> p j n", j=PACK))
             we_raw.append(raw)
         nc.sync.dma_start(wl_w[:], wl_words.bitcast(I32).rearrange("a p c -> p a c"))
@@ -148,8 +155,11 @@ def tile_list_guarantor_loss_rates_kernel(
             else:
                 nc.scalar.activation(dst, banks[t, half][:], ACT.Relu)
 
-        def new_banks():
-            return {(t, half): psum.tile([P, BANK], F32, name="bank") for t in range(PACK) for half in range(S // BANK)}
+        def bank(i, width=BANK):
+            return psum.tile([P, width], F32, name=f"bank{i}", tag=f"bank{i}")
+
+        def new_banks(first):
+            return {(t, half): bank(first[t] + half) for t in range(PACK) for half in range(S // BANK)}
 
         z_w = [tile([P, J], U32, f"z_w{b}") for b in range(RP)]
         z_s = [tile([P, J], U8, f"z_s{b}") for b in range(RP)]
@@ -172,63 +182,124 @@ def tile_list_guarantor_loss_rates_kernel(
         def gather_words(a):
             nc.vector.tensor_copy(v_w[a][:], tab_w[a][:].bitcast(U32).indirect(offs_sb[:]))
 
-        banks = new_banks()
+        def interleave(copy, grouped, raw):
+            copy(grouped.rearrange("p (c i j) -> p c j i", i=4, j=PACK), raw.rearrange("p j (c i) -> p c j i", i=4))
+
+        def quantize_cols(grouped, a, c0, count):
+            codes = tile([P, count * P], U32, f"w1_w{a}0{c0}")
+            scales = tile([P, count * P], U8, f"w1_s{a}0{c0}")
+            quantize(codes[:], scales[:], grouped)
+            for i in range(count):
+                w1_w[a, 0, c0 + i] = codes[:, i * P : (i + 1) * P]
+                w1_s[a, 0, c0 + i] = scales[:, i * P : (i + 1) * P]
+
+        def pick_side(dst, b, t, side, j0, j1):
+            lst = (pos1_sb, pos2_sb)[side]
+            nc.vector.tensor_copy(dst, h[b, t][:].indirect(lst[:, j0 // LANES : j1 // LANES]))
+
+        banks = new_banks((0, 2, 4, 6))
+        v_w[0] = tile([P, S], U32, "v_w0")
         gather_words(0)
         nc.vector.tensor_copy(v_s[:], tab_s[:].bitcast(U8).indirect(offs_sb[:]))
-        gather_words(1)
-        grouped00 = tile([P, WIDE], BF16, "grouped00", tag="slot_a")
-        round_w1(nc.scalar.copy, grouped00[:], 0, 0, 0, 0, PASS)
-        quantize_w1(grouped00[:], 0, 0)
-        for t in range(PACK):
-            layer1_pass(banks, 0, 0, t)
-        v_w.append(tile([P, S], U32, "v_w2", tag="slot_a"))
-        gather_words(2)
+        for a in (0, 1):
+            grouped = tile([P, PACK * HALF], BF16, f"grouped{a}d0")
+            interleave(nc.scalar.copy, grouped[:], w1_raw[a, 0, 0][:])
+            quantize_cols(grouped[:], a, 0, 2)
+            for c in (0, 1):
+                layer1_pass(banks, a, 0, c)
+            v_w[a + 1] = tile([P, S], U32, f"v_w{a + 1}")
+            gather_words(a + 1)
+        grouped = tile([P, PACK * HALF], BF16, "grouped2d0", tag="slot_g")
+        for c in (0, 1):
+            part = grouped[:, c * PASS : (c + 1) * PASS]
+            interleave(nc.scalar.copy, part, w1_raw[2, 0, 0][:, :, c * P : (c + 1) * P])
+            quantize_cols(part, 2, c, 1)
+            layer1_pass(banks, 2, 0, c)
 
-        pair = tile([P, 2 * WIDE - LAP], BF16, "pair")
-        grouped10 = pair[:, WIDE - LAP :]
-        grouped20 = pair[:, :WIDE]
-        round_w1(nc.scalar.copy, grouped10, 1, 0, 0, 0, HALF)
-        round_w1(nc.scalar.copy, grouped10, 1, 0, HALF, HALF, PASS)
-        quantize_w1(grouped10, 1, 0)
-        round_w1(nc.scalar.copy, grouped20, 2, 0, 0, 0, HALF)
-        round_w1(nc.vector.tensor_copy, grouped20, 2, 0, HALF, HALF, PASS)
-        quantize_w1_by_t(grouped20, 2, 0)
+        big = tile([P, 2 * PACK * J + WIDE - LAP], F32, "big", tag="w1_s201")
+        at01 = 0
+        at = WIDE // 2 - LAP // 2
+        plane = {}
+        for key in ((0, 3), (0, 0), (1, 0), (0, 1), (1, 1), (0, 2), (1, 2), (1, 3)):
+            plane[key] = big[:, at : at + J]
+            at += J
+        at21 = at - LAP // 2
+        grouped21 = big[:, at21 : at21 + WIDE // 2].bitcast(BF16)
+        grouped01 = big[:, at01 : at01 + WIDE // 2].bitcast(BF16)
 
-        picked0 = tile([P, 2, PACK, J], F32, "picked0", tag="slot_p")
+        sums = []
 
-        def finish0(t):
-            relu_out(banks, 0, t, 0, False)
-            relu_out(banks, 0, t, 1, t == 0)
-            pick(picked0, 0, t, 0, J)
+        def add_turned(c):
+            for jt in range(J // P):
+                if c == 0:
+                    sums.append(bank(4 + jt))
+                for side in (0, 1):
+                    nc.tensor.matmul(
+                        sums[jt][:, c * P : (c + 1) * P],
+                        plane[side, c][:, jt * P : (jt + 1) * P],
+                        ident[:],
+                        start=(side == 0),
+                        stop=(side == 1),
+                        is_transpose=True,
+                    )
 
-        for t in range(PACK):
-            layer1_pass(banks, 1, 0, t)
-            layer1_pass(banks, 2, 0, t)
-        for t in range(PACK - 1):
-            finish0(t)
+        def relu0(c):
+            relu_out(banks, 0, c, 0, False)
+            relu_out(banks, 0, c, 1, False)
 
-        banks1 = new_banks()
-        grouped01 = tile([P, WIDE], BF16, "grouped01", tag="w1_w201")
-        round_w1(nc.scalar.copy, grouped01[:], 0, 1, 0, 0, PASS)
-        quantize_w1(grouped01[:], 0, 1)
-        finish0(PACK - 1)
-        for t in range(PACK):
+        grouped = tile([P, PACK * HALF], BF16, "grouped0d1", tag="slot_g")
+        interleave(nc.vector.tensor_copy, grouped[:], w1_raw[0, 0, HALF][:])
+        quantize_cols(grouped[:], 0, 2, 2)
+        relu0(0)
+        pick_side(plane[0, 0], 0, 0, 0, 0, J)
+        pick_side(plane[1, 0], 0, 0, 1, 0, J)
+        relu0(1)
+        for c in (2, 3):
+            layer1_pass(banks, 0, 0, c)
+        grouped = plane[0, 1].bitcast(BF16)
+        interleave(nc.scalar.copy, grouped, w1_raw[1, 0, HALF][:])
+        quantize_cols(grouped, 1, 2, 2)
+        pick_side(plane[0, 1], 0, 1, 0, 0, J)
+        grouped = plane[1, 1].bitcast(BF16)
+        for c in (2, 3):
+            part = grouped[:, (c - 2) * PASS : (c - 1) * PASS]
+            interleave(nc.scalar.copy, part, w1_raw[2, 0, HALF][:, :, (c - 2) * P : (c - 1) * P])
+            quantize_cols(part, 2, c, 1)
+            layer1_pass(banks, 1, 0, c)
+            layer1_pass(banks, 2, 0, c)
+        pick_side(plane[1, 1], 0, 1, 1, 0, J)
+        relu0(2)
+        pick_side(plane[0, 2], 0, 2, 0, 0, J)
+        pick_side(plane[1, 2], 0, 2, 1, 0, J)
+        relu0(3)
+        add_turned(0)
+        add_turned(1)
+
+        banks1 = new_banks((0, 2, 0, 2))
+        round_w1(nc.scalar.copy, grouped01, 0, 1, 0, 0, HALF)
+        round_w1(nc.scalar.copy, grouped01, 0, 1, HALF, HALF, PASS)
+        quantize_w1(grouped01, 0, 1)
+        pick_side(plane[0, 3], 0, 3, 0, 0, J)
+        for t in (0, 1):
             layer1_pass(banks1, 0, 1, t)
-
-        both11 = tile([P, WIDE + WIDE // 2 - LAP], BF16, "both11", tag="w1_w202")
-        round_w1(nc.scalar.copy, both11[:, :WIDE], 1, 1, 0, 0, PASS)
-        quantize_w1(both11[:, :WIDE], 1, 1)
-        both21 = tile([P, WIDE + WIDE // 2 - LAP], BF16, "both21", tag="w1_w203")
-        round_w1(nc.scalar.copy, both21[:, :WIDE], 2, 1, 0, 0, PASS)
-        quantize_w1_by_t(both21[:, :WIDE], 2, 1)
-        add_z(both11[:, WIDE - LAP :], picked0, 0, J // 2)
-        add_z(both21[:, WIDE - LAP :], picked0, J // 2, J)
-        quantize_z(both11[:, WIDE - LAP :], 0, 0, J // 2)
-        quantize_z(both21[:, WIDE - LAP :], 0, J // 2, J)
+        grouped11 = tile([P, WIDE], BF16, "grouped11", tag="w1_w200")
+        round_w1(nc.scalar.copy, grouped11[:], 1, 1, 0, 0, PASS)
+        quantize_w1(grouped11[:], 1, 1)
+        round_w1(nc.scalar.copy, grouped21, 2, 1, 0, 0, HALF)
+        round_w1(nc.vector.tensor_copy, grouped21, 2, 1, 0, HALF, PASS)
+        codes21 = tile([P, PASS], U32, "w1_w21", tag="w1_w200")
+        scales21 = tile([P, PASS], U8, "w1_s21")
+        for t in range(PACK):
+            cols = slice(t * P, (t + 1) * P)
+            quantize(codes21[:, cols], scales21[:, cols], grouped21[:, t * PASS : (t + 1) * PASS])
+            w1_w[2, 1, t], w1_s[2, 1, t] = codes21[:, cols], scales21[:, cols]
+        pick_side(plane[1, 3], 0, 3, 1, 0, J)
 
         z_bf1 = tile([P, J * PACK], BF16, "z_bf1")
-        picked = tile([P, 2, PACK, 2 * UNIT], F32, "picked10", tag="slot_p")
+        picked = tile([P, 2, PACK, 2 * UNIT], F32, "picked10", tag="tab_w1")
         for t in range(PACK):
+            if t >= 2:
+                layer1_pass(banks1, 0, 1, t)
             layer1_pass(banks1, 1, 1, t)
             layer1_pass(banks1, 2, 1, t)
             relu_out(banks1, 1, t, 0, False)
@@ -237,60 +308,116 @@ def tile_list_guarantor_loss_rates_kernel(
         add_z(z_bf1[:, : 2 * UNIT * PACK], picked, 0, 2 * UNIT)
         quantize_z(z_bf1[:, : 2 * UNIT * PACK], 1, 0, 2 * UNIT)
 
+        add_turned(2)
+        add_turned(3)
+        z_t = tile([P, J // P, PASS], BF16, "z_t", tag="tab_w0")
+
+        def round_z(jt):
+            nc.scalar.copy(
+                z_t[:, jt, :].rearrange("j (u p e) -> j u p e", u=2, e=2),
+                sums[jt][:].rearrange("j (p u e) -> j u p e", u=2, e=2),
+            )
+
+        def turn_back(jp):
+            z_bf0 = tile([P, 2 * P * PACK], BF16, f"z_bf0{jp}")
+            back = bank(4 + 2 * jp)
+            for i in range(2):
+                words = z_t[:, 2 * jp + i, :].bitcast(F32)
+                for u in range(2):
+                    nc.tensor.transpose(
+                        back[:, (2 * i + u) * P : (2 * i + u + 1) * P], words[:, u * P : (u + 1) * P], ident[:]
+                    )
+            nc.scalar.copy(
+                z_bf0[:].bitcast(F32).rearrange("p (i j u) -> p i j u", i=2, u=2),
+                back[:].rearrange("p (i u j) -> p i j u", i=2, u=2),
+            )
+            quantize_z(z_bf0[:], 0, jp * 2 * P, (jp + 1) * 2 * P)
+
         we_w = [tile([P, N], U32, f"we_w{b}") for b in range(RP)]
         we_s = [tile([P, N], U8, f"we_s{b}") for b in range(RP)]
-        for b in range(RP):
-            grouped = tile([P, N * PACK], BF16, f"grouped_we{b}", tag=f"w1_s20{3 - b}")
-            for n0 in (0, N // 2):
-                nc.scalar.copy(
-                    grouped[:, PACK * n0 : PACK * (n0 + N // 2)].rearrange("p (c i j) -> p c j i", i=4, j=PACK),
-                    we_raw[b][:, :, n0 : n0 + N // 2].rearrange("p j (c i) -> p c j i", i=4),
-                )
+
+        def quantize_we(b, width):
+            grouped = tile([P, N * PACK], BF16, f"grouped_we{b}", tag=("w1_s200", "w1_w201")[b])
+            for n0 in range(0, N, width):
+                interleave(nc.scalar.copy, grouped[:, PACK * n0 : PACK * (n0 + width)], we_raw[b][:, :, n0 : n0 + width])
             quantize(we_w[b][:], we_s[b][:], grouped[:])
 
         out_v = out.rearrange("(nt p) j -> p nt j", p=P)
 
-        def heads(u):
+        def head(bank, weights, fmt, bytes_per_col, u, nts):
             cols = slice(u * UNIT, (u + 1) * UNIT)
-            expo = psum.tile([P, BANK], F32, name="bank")
-            loss = psum.tile([P, BANK], F32, name="bank")
-            for nt in range(NT):
+            for i, nt in enumerate(nts):
                 for b in range(RP):
+                    words, scales = weights[b]
                     nc.tensor.matmul_mx(
-                        out=expo[:, nt * UNIT : (nt + 1) * UNIT],
-                        lhsT=we_w[b][:, nt * P : (nt + 1) * P].bitcast(FP8X4),
-                        lhsT_scale=we_s[b][:, nt * P : (nt + 1) * P],
+                        out=bank[:, i * UNIT : (i + 1) * UNIT],
+                        lhsT=words[:, bytes_per_col * nt * P : bytes_per_col * (nt + 1) * P].bitcast(fmt),
+                        lhsT_scale=scales[:, nt * P : (nt + 1) * P],
                         rhs=z_w[b][:, cols].bitcast(FP8X4),
                         rhs_scale=z_s[b][:, cols],
                         start=(b == 0),
                         stop=(b == RP - 1),
                     )
-            for nt in range(NT):
-                for b in range(RP):
-                    nc.tensor.matmul_mx(
-                        out=loss[:, nt * UNIT : (nt + 1) * UNIT],
-                        lhsT=wl_w[:, b, :].bitcast(U8)[:, 2 * nt * P : 2 * (nt + 1) * P].bitcast(FP4X4),
-                        lhsT_scale=wl_s[:, b, :].bitcast(U8)[:, nt * P : (nt + 1) * P],
-                        rhs=z_w[b][:, cols].bitcast(FP8X4),
-                        rhs_scale=z_s[b][:, cols],
-                        start=(b == 0),
-                        stop=(b == RP - 1),
-                    )
-            size = ring.tile([P, BANK], F32, name="size")
-            root = ring.tile([P, BANK], F32, name="root")
-            score = keep.tile([P, BANK], F32, name=f"score{u}")
+
+        we_mx = [(we_w[b][:].bitcast(U8), we_s[b][:]) for b in range(RP)]
+        wl_mx = [(wl_w[:, b, :].bitcast(U8), wl_s[:, b, :].bitcast(U8)) for b in range(RP)]
+        spare = ["tab_w2", "w1_raw010", "w1_raw110", "w1_raw210", "we_raw0"]
+
+        def exposure(u, nts, square, size=None):
+            width = len(nts) * UNIT
+            expo = bank({(0, 0): 0, (1, 0): 1, (2, 0): 5, (3, 0): 0, (3, 2): 4}[u, nts[0]], width)
+            head(expo, we_mx, FP8X4, 4, u, nts)
+            if size is None:
+                size = tile([P, width], F32, f"size{u}{nts[0]}")
+            root = tile([P, width], F32, f"root{u}{nts[0]}", tag=spare.pop(0))
             nc.scalar.activation(size[:], expo[:], ACT.Abs)
             nc.scalar.activation(root[:], size[:], ACT.Abs_reciprocal_sqrt, bias=1.0)
-            nc.scalar.activation(size[:], root[:], ACT.Square)
-            nc.vector.tensor_tensor(score[:], loss[:], size[:], ALU.mult)
-            nc.sync.dma_start(out_v[:, :, cols], score[:].rearrange("p (nt j) -> p nt j", nt=NT))
+            if square:
+                nc.scalar.activation(size[:], root[:], ACT.Square)
+            return size, root
 
-        for u in (2, 3):
+        def finish(u, nts, square, size, root):
+            width = len(nts) * UNIT
+            loss = bank({(0, 0): 2, (1, 0): 3, (2, 0): 7, (3, 0): 1, (3, 2): 6}[u, nts[0]], width)
+            head(loss, wl_mx, FP4X4, 2, u, nts)
+            score = tile([P, width], F32, f"score{u}{nts[0]}")
+            if square:
+                nc.vector.tensor_tensor(score[:], loss[:], size[:], ALU.mult)
+            else:
+                nc.vector.tensor_tensor(size[:], loss[:], root[:], ALU.mult)
+                nc.vector.tensor_tensor(score[:], size[:], root[:], ALU.mult)
+            nc.sync.dma_start(
+                out_v[:, nts[0] : nts[-1] + 1, u * UNIT : (u + 1) * UNIT],
+                score[:].rearrange("p (nt j) -> p nt j", j=UNIT),
+            )
+
+        def last_picks(u, tag):
             j0, j1 = u * UNIT, (u + 1) * UNIT
-            picked = tile([P, 2, PACK, UNIT], F32, f"picked1{u}", tag="w1_s202")
+            picked = tile([P, 2, PACK, UNIT], F32, f"picked1{u}", tag=tag)
             for t in range(PACK):
                 pick(picked, 1, t, j0, j1)
             add_z(z_bf1[:, j0 * PACK : j1 * PACK], picked, 0, UNIT)
             quantize_z(z_bf1[:, j0 * PACK : j1 * PACK], 1, j0, j1)
-        for u in range(J // UNIT):
-            heads(u)
+
+        every = (0, 1, 2, 3)
+        quantize_we(0, P)
+        round_z(0)
+        round_z(1)
+        quantize_we(1, N // 2)
+        turn_back(0)
+        round_z(2)
+        round_z(3)
+        last_picks(2, "w1_w201")
+        e0 = exposure(0, every, True)
+        turn_back(1)
+        e1 = exposure(1, every, True)
+        last_picks(3, "z_bf01")
+        finish(0, every, True, *e0)
+        finish(1, every, True, *e1)
+        e2 = exposure(2, every, True)
+        finish(2, every, True, *e2)
+        size3 = tile([P, BANK], F32, "size3", tag="w1_raw110")
+        e3 = exposure(3, (0, 1), True, size3[:, : 2 * UNIT])
+        e4 = exposure(3, (2, 3), True, size3[:, 2 * UNIT :])
+        finish(3, (0, 1), True, *e3)
+        finish(3, (2, 3), True, *e4)

from contextlib import ExitStack

import concourse.mybir as mybir
from concourse.masks import make_identity

K, H, N, T, S, J = 1536, 1024, 512, 2048, 1024, 512
FLOPS = 2 * K * H * S + 2 * 2 * H * N * J

F32 = mybir.dt.float32
BF16 = mybir.dt.bfloat16
I32 = mybir.dt.int32
U32 = mybir.dt.uint32
U16 = mybir.dt.uint16
U8 = mybir.dt.uint8
FP8X4 = mybir.dt.float8_e4m3fn_x4
FP4X4 = mybir.dt.float4_e2m1fn_x4
ACT = mybir.ActivationFunctionType
ALU = mybir.AluOpType

P = 128
PACK = 4
PASS = P * PACK
BANK = 512
KP = K // PASS
RP = H // PASS
NT = N // P
UNIT = 128
LANES = 16
HALF = PASS // 2
WIDE = PASS * PACK
LAP = 32


def tile_list_guarantor_loss_rates_kernel(
    tc, tab_words, tab_scales, offs, pos1, pos2, w1, wl_words, wl_scales, we, out
):
    nc = tc.nc
    with ExitStack() as ctx:
        keep = ctx.enter_context(tc.tile_pool(name="keep", bufs=1))
        ring = ctx.enter_context(tc.tile_pool(name="ring", bufs=2))
        psum = ctx.enter_context(tc.psum_pool(name="psum", bufs=1))

        offs_sb = keep.tile([P, S // LANES], U16, name="offs_sb")
        pos1_sb = keep.tile([P, J // LANES], U16, name="pos1_sb")
        pos2_sb = keep.tile([P, J // LANES], U16, name="pos2_sb")

        tab_w = [keep.tile([P, T], I32, name=f"tab_w{a}", tag=f"tab_w{a}", align_bytes=64) for a in range(KP)]
        tab_s = keep.tile([P, T // 4], I32, name="tab_s")
        v_w = {}
        v_s = keep.tile([P, S], U8, name="v_s", align_bytes=64)

        wl_w = keep.tile([P, RP, N // 2], I32, name="wl_w", align_bytes=64)
        wl_s = keep.tile([P, RP, N // 4], I32, name="wl_s", align_bytes=64)

        nc.vector.memset(tab_s[:], 0)
        nc.vector.memset(wl_s[:], 0)

        def load_tab(a):
            nc.sync.dma_start(tab_w[a][:], tab_words[a].rearrange("p n i -> p (n i)").bitcast(I32))

        w1_raw = {}

        def load_w1(a, b, c0, c1):
            raw = keep.tile([P, PACK, c1 - c0], F32, name=f"w1_raw{a}{b}{c0}", tag=f"w1_raw{a}{b}{c0}", align_bytes=64)
            src = w1[a * PASS : (a + 1) * PASS, b * PASS + c0 : b * PASS + c1]
            nc.sync.dma_start(raw[:], src.rearrange("(p j) c -> p j c", j=PACK))
            w1_raw[a, b, c0] = raw

        load_tab(0)
        nc.sync.dma_start(offs_sb[:], offs)
        for q in range(4):
            (nc.sync, nc.scalar)[q % 2].dma_start(
                tab_s[32 * q : 32 * q + 4 * KP, :], tab_scales[:, 4 * q : 4 * q + 4, :].bitcast(I32)
            )
        warm_in = keep.tile([P, 1], F32, name="warm_in")
        warm_out = keep.tile([P, 1], F32, name="warm_out")
        nc.vector.memset(warm_in[:], 1.0)
        nc.scalar.activation(warm_out[:], warm_in[:], ACT.Abs_reciprocal_sqrt)
        ident = keep.tile([P, P], F32, name="ident")
        make_identity(nc, ident[:])
        load_w1(0, 0, 0, HALF)
        load_tab(1)
        load_w1(1, 0, 0, HALF)
        load_tab(2)
        load_w1(2, 0, 0, HALF)
        load_w1(0, 0, HALF, PASS)
        nc.sync.dma_start(pos1_sb[:], pos1)
        nc.sync.dma_start(pos2_sb[:], pos2)
        load_w1(1, 0, HALF, PASS)
        load_w1(2, 0, HALF, PASS)
        load_w1(0, 1, 0, HALF)
        load_w1(0, 1, HALF, PASS)
        load_w1(1, 1, 0, PASS)
        load_w1(2, 1, 0, PASS)
        we_raw = []
        for b in range(RP):
            raw = keep.tile([P, PACK, N], F32, name=f"we_raw{b}", tag=f"we_raw{b}", align_bytes=64)
            nc.sync.dma_start(raw[:], we[b * PASS : (b + 1) * PASS, :].rearrange("(p j) n -> p j n", j=PACK))
            we_raw.append(raw)
        nc.sync.dma_start(wl_w[:], wl_words.bitcast(I32).rearrange("a p c -> p a c"))
        for q in range(4):
            nc.sync.dma_start(
                wl_s[32 * q : 32 * q + 4, :, :],
                wl_scales[:, 4 * q : 4 * q + 4, :].bitcast(I32).rearrange("a i c -> i a c"),
            )

        def tile(shape, dtype, name, tag=None):
            return keep.tile(shape, dtype, name=name, tag=tag or name, align_bytes=64)

        h = {(b, t): tile([P, S], F32, f"h{b}{t}") for b in range(RP) for t in range(PACK)}
        w1_w, w1_s = {}, {}

        def quantize(codes, scales, src):
            nc.vector.quantize_mx(out=codes.bitcast(FP8X4), scales=scales, in_=src)

        def round_w1(copy, grouped, a, b, c0, lo, hi):
            raw = w1_raw[a, b, c0]
            copy(
                grouped.rearrange("p (t m j) -> p m j t", t=PACK, j=PACK)[:, lo // PACK : hi // PACK],
                raw[:, :, lo - c0 : hi - c0].rearrange("p j (m t) -> p m j t", t=PACK),
            )

        def quantize_w1(grouped, a, b):
            codes = tile([P, PASS], U32, f"w1_w{a}{b}")
            scales = tile([P, PASS], U8, f"w1_s{a}{b}")
            quantize(codes[:], scales[:], grouped)
            for t in range(PACK):
                w1_w[a, b, t] = codes[:, t * P : (t + 1) * P]
                w1_s[a, b, t] = scales[:, t * P : (t + 1) * P]

        def quantize_w1_by_t(grouped, a, b):
            for t in range(PACK):
                codes = tile([P, P], U32, f"w1_w{a}{b}{t}")
                scales = tile([P, P], U8, f"w1_s{a}{b}{t}")
                quantize(codes[:], scales[:], grouped[:, t * PASS : (t + 1) * PASS])
                w1_w[a, b, t], w1_s[a, b, t] = codes[:], scales[:]

        def layer1_pass(banks, a, b, t):
            for half in range(S // BANK):
                ent = slice(half * BANK, (half + 1) * BANK)
                nc.tensor.matmul_mx(
                    out=banks[t, half][:],
                    lhsT=w1_w[a, b, t].bitcast(FP8X4),
                    lhsT_scale=w1_s[a, b, t],
                    rhs=v_w[a][:, ent].bitcast(FP8X4),
                    rhs_scale=v_s[4 * a : P, ent],
                    start=(a == 0),
                    stop=(a == KP - 1),
                )

        def relu_out(banks, b, t, half, on_vector):
            dst = h[b, t][:, half * BANK : (half + 1) * BANK]
            if on_vector:
                nc.vector.tensor_scalar_max(dst, banks[t, half][:], 0.0)
            else:
                nc.scalar.activation(dst, banks[t, half][:], ACT.Relu)

        def bank(i, width=BANK):
            return psum.tile([P, width], F32, name=f"bank{i}", tag=f"bank{i}")

        def new_banks(first):
            return {(t, half): bank(first[t] + half) for t in range(PACK) for half in range(S // BANK)}

        z_w = [tile([P, J], U32, f"z_w{b}") for b in range(RP)]
        z_s = [tile([P, J], U8, f"z_s{b}") for b in range(RP)]

        def pick(picked, b, t, j0, j1):
            for side, lst in enumerate((pos1_sb, pos2_sb)):
                nc.vector.tensor_copy(picked[:, side, t, :], h[b, t][:].indirect(lst[:, j0 // LANES : j1 // LANES]))

        def add_z(z_bf, picked, c0, c1):
            nc.vector.tensor_tensor(
                z_bf.rearrange("p (c i t) -> p c t i", i=4, t=PACK),
                picked[:, 0, :, c0:c1].rearrange("p t (c i) -> p c t i", i=4),
                picked[:, 1, :, c0:c1].rearrange("p t (c i) -> p c t i", i=4),
                ALU.add,
            )

        def quantize_z(z_bf, b, j0, j1):
            quantize(z_w[b][:, j0:j1], z_s[b][:, j0:j1], z_bf)

        def gather_words(a):
            nc.vector.tensor_copy(v_w[a][:], tab_w[a][:].bitcast(U32).indirect(offs_sb[:]))

        def interleave(copy, grouped, raw):
            copy(grouped.rearrange("p (c i j) -> p c j i", i=4, j=PACK), raw.rearrange("p j (c i) -> p c j i", i=4))

        def quantize_cols(grouped, a, c0, count):
            codes = tile([P, count * P], U32, f"w1_w{a}0{c0}")
            scales = tile([P, count * P], U8, f"w1_s{a}0{c0}")
            quantize(codes[:], scales[:], grouped)
            for i in range(count):
                w1_w[a, 0, c0 + i] = codes[:, i * P : (i + 1) * P]
                w1_s[a, 0, c0 + i] = scales[:, i * P : (i + 1) * P]

        def pick_side(dst, b, t, side, j0, j1):
            lst = (pos1_sb, pos2_sb)[side]
            nc.vector.tensor_copy(dst, h[b, t][:].indirect(lst[:, j0 // LANES : j1 // LANES]))

        banks = new_banks((0, 2, 4, 6))
        v_w[0] = tile([P, S], U32, "v_w0")
        gather_words(0)
        nc.vector.tensor_copy(v_s[:], tab_s[:].bitcast(U8).indirect(offs_sb[:]))
        for a in (0, 1):
            grouped = tile([P, PACK * HALF], BF16, f"grouped{a}d0")
            interleave(nc.scalar.copy, grouped[:], w1_raw[a, 0, 0][:])
            quantize_cols(grouped[:], a, 0, 2)
            for c in (0, 1):
                layer1_pass(banks, a, 0, c)
            v_w[a + 1] = tile([P, S], U32, f"v_w{a + 1}")
            gather_words(a + 1)
        grouped = tile([P, PACK * HALF], BF16, "grouped2d0", tag="slot_g")
        for c in (0, 1):
            part = grouped[:, c * PASS : (c + 1) * PASS]
            interleave(nc.scalar.copy, part, w1_raw[2, 0, 0][:, :, c * P : (c + 1) * P])
            quantize_cols(part, 2, c, 1)
            layer1_pass(banks, 2, 0, c)

        big = tile([P, 2 * PACK * J + WIDE - LAP], F32, "big", tag="w1_s201")
        at01 = 0
        at = WIDE // 2 - LAP // 2
        plane = {}
        for key in ((0, 3), (0, 0), (1, 0), (0, 1), (1, 1), (0, 2), (1, 2), (1, 3)):
            plane[key] = big[:, at : at + J]
            at += J
        at21 = at - LAP // 2
        grouped21 = big[:, at21 : at21 + WIDE // 2].bitcast(BF16)
        grouped01 = big[:, at01 : at01 + WIDE // 2].bitcast(BF16)

        sums = []

        def add_turned(c):
            for jt in range(J // P):
                if c == 0:
                    sums.append(bank(4 + jt))
                for side in (0, 1):
                    nc.tensor.matmul(
                        sums[jt][:, c * P : (c + 1) * P],
                        plane[side, c][:, jt * P : (jt + 1) * P],
                        ident[:],
                        start=(side == 0),
                        stop=(side == 1),
                        is_transpose=True,
                    )

        def relu0(c):
            relu_out(banks, 0, c, 0, False)
            relu_out(banks, 0, c, 1, False)

        grouped = tile([P, PACK * HALF], BF16, "grouped0d1", tag="slot_g")
        interleave(nc.vector.tensor_copy, grouped[:], w1_raw[0, 0, HALF][:])
        quantize_cols(grouped[:], 0, 2, 2)
        relu0(0)
        pick_side(plane[0, 0], 0, 0, 0, 0, J)
        pick_side(plane[1, 0], 0, 0, 1, 0, J)
        relu0(1)
        for c in (2, 3):
            layer1_pass(banks, 0, 0, c)
        grouped = plane[0, 1].bitcast(BF16)
        interleave(nc.scalar.copy, grouped, w1_raw[1, 0, HALF][:])
        quantize_cols(grouped, 1, 2, 2)
        pick_side(plane[0, 1], 0, 1, 0, 0, J)
        grouped = plane[1, 1].bitcast(BF16)
        for c in (2, 3):
            part = grouped[:, (c - 2) * PASS : (c - 1) * PASS]
            interleave(nc.scalar.copy, part, w1_raw[2, 0, HALF][:, :, (c - 2) * P : (c - 1) * P])
            quantize_cols(part, 2, c, 1)
            layer1_pass(banks, 1, 0, c)
            layer1_pass(banks, 2, 0, c)
        pick_side(plane[1, 1], 0, 1, 1, 0, J)
        relu0(2)
        pick_side(plane[0, 2], 0, 2, 0, 0, J)
        pick_side(plane[1, 2], 0, 2, 1, 0, J)
        relu0(3)
        add_turned(0)
        add_turned(1)

        banks1 = new_banks((0, 2, 0, 2))
        round_w1(nc.scalar.copy, grouped01, 0, 1, 0, 0, HALF)
        round_w1(nc.scalar.copy, grouped01, 0, 1, HALF, HALF, PASS)
        quantize_w1(grouped01, 0, 1)
        pick_side(plane[0, 3], 0, 3, 0, 0, J)
        for t in (0, 1):
            layer1_pass(banks1, 0, 1, t)
        grouped11 = tile([P, WIDE], BF16, "grouped11", tag="w1_w200")
        round_w1(nc.scalar.copy, grouped11[:], 1, 1, 0, 0, PASS)
        quantize_w1(grouped11[:], 1, 1)
        round_w1(nc.scalar.copy, grouped21, 2, 1, 0, 0, HALF)
        round_w1(nc.vector.tensor_copy, grouped21, 2, 1, 0, HALF, PASS)
        codes21 = tile([P, PASS], U32, "w1_w21", tag="w1_w200")
        scales21 = tile([P, PASS], U8, "w1_s21")
        for t in range(PACK):
            cols = slice(t * P, (t + 1) * P)
            quantize(codes21[:, cols], scales21[:, cols], grouped21[:, t * PASS : (t + 1) * PASS])
            w1_w[2, 1, t], w1_s[2, 1, t] = codes21[:, cols], scales21[:, cols]
        pick_side(plane[1, 3], 0, 3, 1, 0, J)

        z_bf1 = tile([P, J * PACK], BF16, "z_bf1")
        picked = tile([P, 2, PACK, 2 * UNIT], F32, "picked10", tag="tab_w1")
        for t in range(PACK):
            if t >= 2:
                layer1_pass(banks1, 0, 1, t)
            layer1_pass(banks1, 1, 1, t)
            layer1_pass(banks1, 2, 1, t)
            relu_out(banks1, 1, t, 0, False)
            relu_out(banks1, 1, t, 1, False)
            pick(picked, 1, t, 0, 2 * UNIT)
        add_z(z_bf1[:, : 2 * UNIT * PACK], picked, 0, 2 * UNIT)
        quantize_z(z_bf1[:, : 2 * UNIT * PACK], 1, 0, 2 * UNIT)

        add_turned(2)
        add_turned(3)
        z_t = tile([P, J // P, PASS], BF16, "z_t", tag="tab_w0")

        def round_z(jt):
            nc.scalar.copy(
                z_t[:, jt, :].rearrange("j (u p e) -> j u p e", u=2, e=2),
                sums[jt][:].rearrange("j (p u e) -> j u p e", u=2, e=2),
            )

        def turn_back(jp):
            z_bf0 = tile([P, 2 * P * PACK], BF16, f"z_bf0{jp}")
            back = bank(4 + 2 * jp)
            for i in range(2):
                words = z_t[:, 2 * jp + i, :].bitcast(F32)
                for u in range(2):
                    nc.tensor.transpose(
                        back[:, (2 * i + u) * P : (2 * i + u + 1) * P], words[:, u * P : (u + 1) * P], ident[:]
                    )
            nc.scalar.copy(
                z_bf0[:].bitcast(F32).rearrange("p (i j u) -> p i j u", i=2, u=2),
                back[:].rearrange("p (i u j) -> p i j u", i=2, u=2),
            )
            quantize_z(z_bf0[:], 0, jp * 2 * P, (jp + 1) * 2 * P)

        we_w = [tile([P, N], U32, f"we_w{b}") for b in range(RP)]
        we_s = [tile([P, N], U8, f"we_s{b}") for b in range(RP)]

        def quantize_we(b, width):
            grouped = tile([P, N * PACK], BF16, f"grouped_we{b}", tag=("w1_s200", "w1_w201")[b])
            for n0 in range(0, N, width):
                interleave(nc.scalar.copy, grouped[:, PACK * n0 : PACK * (n0 + width)], we_raw[b][:, :, n0 : n0 + width])
            quantize(we_w[b][:], we_s[b][:], grouped[:])

        out_v = out.rearrange("(nt p) j -> p nt j", p=P)

        def head(bank, weights, fmt, bytes_per_col, u, nts):
            cols = slice(u * UNIT, (u + 1) * UNIT)
            for i, nt in enumerate(nts):
                for b in range(RP):
                    words, scales = weights[b]
                    nc.tensor.matmul_mx(
                        out=bank[:, i * UNIT : (i + 1) * UNIT],
                        lhsT=words[:, bytes_per_col * nt * P : bytes_per_col * (nt + 1) * P].bitcast(fmt),
                        lhsT_scale=scales[:, nt * P : (nt + 1) * P],
                        rhs=z_w[b][:, cols].bitcast(FP8X4),
                        rhs_scale=z_s[b][:, cols],
                        start=(b == 0),
                        stop=(b == RP - 1),
                    )

        we_mx = [(we_w[b][:].bitcast(U8), we_s[b][:]) for b in range(RP)]
        wl_mx = [(wl_w[:, b, :].bitcast(U8), wl_s[:, b, :].bitcast(U8)) for b in range(RP)]
        spare = ["tab_w2", "w1_raw010", "w1_raw110", "w1_raw210", "we_raw0"]

        def exposure(u, nts, square, size=None):
            width = len(nts) * UNIT
            expo = bank({(0, 0): 0, (1, 0): 1, (2, 0): 5, (3, 0): 0, (3, 2): 4}[u, nts[0]], width)
            head(expo, we_mx, FP8X4, 4, u, nts)
            if size is None:
                size = tile([P, width], F32, f"size{u}{nts[0]}")
            root = tile([P, width], F32, f"root{u}{nts[0]}", tag=spare.pop(0))
            nc.scalar.activation(size[:], expo[:], ACT.Abs)
            nc.scalar.activation(root[:], size[:], ACT.Abs_reciprocal_sqrt, bias=1.0)
            if square:
                nc.scalar.activation(size[:], root[:], ACT.Square)
            return size, root

        def finish(u, nts, square, size, root):
            width = len(nts) * UNIT
            loss = bank({(0, 0): 2, (1, 0): 3, (2, 0): 7, (3, 0): 1, (3, 2): 6}[u, nts[0]], width)
            head(loss, wl_mx, FP4X4, 2, u, nts)
            score = tile([P, width], F32, f"score{u}{nts[0]}")
            if square:
                nc.vector.tensor_tensor(score[:], loss[:], size[:], ALU.mult)
            else:
                nc.vector.tensor_tensor(size[:], loss[:], root[:], ALU.mult)
                nc.vector.tensor_tensor(score[:], size[:], root[:], ALU.mult)
            nc.sync.dma_start(
                out_v[:, nts[0] : nts[-1] + 1, u * UNIT : (u + 1) * UNIT],
                score[:].rearrange("p (nt j) -> p nt j", j=UNIT),
            )

        def last_picks(u, tag):
            j0, j1 = u * UNIT, (u + 1) * UNIT
            picked = tile([P, 2, PACK, UNIT], F32, f"picked1{u}", tag=tag)
            for t in range(PACK):
                pick(picked, 1, t, j0, j1)
            add_z(z_bf1[:, j0 * PACK : j1 * PACK], picked, 0, UNIT)
            quantize_z(z_bf1[:, j0 * PACK : j1 * PACK], 1, j0, j1)

        every = (0, 1, 2, 3)
        quantize_we(0, P)
        round_z(0)
        round_z(1)
        quantize_we(1, N // 2)
        turn_back(0)
        round_z(2)
        round_z(3)
        last_picks(2, "w1_w201")
        e0 = exposure(0, every, True)
        turn_back(1)
        e1 = exposure(1, every, True)
        last_picks(3, "z_bf01")
        finish(0, every, True, *e0)
        finish(1, every, True, *e1)
        e2 = exposure(2, every, True)
        finish(2, every, True, *e2)
        size3 = tile([P, BANK], F32, "size3", tag="w1_raw110")
        e3 = exposure(3, (0, 1), True, size3[:, : 2 * UNIT])
        e4 = exposure(3, (2, 3), True, size3[:, 2 * UNIT :])
        finish(3, (0, 1), True, *e3)
        finish(3, (2, 3), True, *e4)
